import numpy as np
import ml_dtypes


def mxq(x, axis, fmt="e4m3"):
    dtype, down = {"e4m3": (ml_dtypes.float8_e4m3fn, 7), "e5m2": (ml_dtypes.float8_e5m2, 14)}[fmt]
    v = np.moveaxis(np.asarray(x, np.float32).astype(ml_dtypes.bfloat16).astype(np.float64), axis, -1)
    blocks = v.reshape(v.shape[:-1] + (-1, 32))
    amax = np.abs(blocks).max(-1, keepdims=True)
    byte = np.maximum(np.where(amax > 0, np.frexp(amax)[1] - 1 + 127, 0) - down, 1)
    scale = np.exp2(byte - 127.0)
    codes = (blocks / scale).astype(np.float32).astype(dtype).astype(np.float64)
    return np.moveaxis((codes * scale).reshape(v.shape), -1, axis)


WIDE = False


def mx_kscale(k):
    if not WIDE:
        return np.ones(k)
    levels = np.array([10, -10, 5, -5, 0])
    if k % 512:
        return np.exp2(np.random.permutation(np.resize(levels, k // 32))).repeat(32)
    a = np.empty((k // 512, 16))
    for p in range(k // 512):
        a[p, :8] = np.random.permutation(np.resize(levels, 8))
        for g in range(8):
            far = levels[np.abs(levels - a[p, g]) >= 10]
            a[p, g + 8] = far[np.random.randint(len(far))]
    return np.exp2(a.ravel()).repeat(32)


BF16 = ml_dtypes.bfloat16


def bf(x):
    return np.asarray(x, np.float32).astype(BF16)


def f64(x):
    return np.asarray(x).astype(np.float64)

def planes(Y):
    n, m = Y.shape
    b = f64(bf(Y)).reshape(n // 32, 32, m)
    amax = np.abs(b).max(1)
    byte = np.clip(np.where(amax > 0, np.frexp(amax)[1] - 1 + 127 - 7, 1), 1, 254)
    codes = (b * np.exp2(127.0 - byte)[:, None, :]).reshape(n, m).astype(np.float32).astype(ml_dtypes.float8_e4m3fn).view(np.uint8)
    words = codes.reshape(n // 512, 128, 4, m).transpose(0, 1, 3, 2)
    return np.ascontiguousarray(words), np.ascontiguousarray(byte.astype(np.uint8).reshape(n // 512, 16, m))


T, D, E, R, F = 1024, 512, 4, 512, 512


def expert_scores(a):
    return np.sqrt(np.sum(a * a, axis=-1))


def silu(v):
    return v / (1.0 + np.exp(-v))


def softmax_experts(score):
    e = np.exp(score - score.max(axis=0, keepdims=True))
    return e / e.sum(axis=0, keepdims=True)


def setup_inputs():
    s, t = mx_kscale(D), mx_kscale(R)
    return {"x": bf(np.random.standard_normal((T, D)) * s),
            "wdown": bf(np.random.standard_normal((E, D, R)) / np.sqrt(D) / s[None, :, None]),
            "rgain": bf((1.0 + 0.1 * np.random.standard_normal((E, R))) * t),
            "wup": bf(np.random.standard_normal((E, R, F)) * 1.5 / np.sqrt(R) / t[None, :, None]),
            "wp": bf(np.random.standard_normal((E, D, F)) / np.sqrt(D) / s[None, :, None])}


def core(x, wdown, rgain, wup, wp):
    xq = mxq(f64(x), 1, "e4m3")
    a = xq @ mxq(f64(wdown), 1, "e4m3")
    score = expert_scores(a)
    g = softmax_experts(score)
    b = a * f64(rgain)[:, None, :]
    u = mxq(b, 2, "e4m3") @ mxq(f64(wup), 1, "e4m3")
    p = xq @ mxq(f64(wp), 1, "e4m3")
    return np.sum(g[:, :, None] * silu(u) * p, axis=0)


def reference(x, wdown, rgain, wup, wp):
    R_out = core(x, wdown, rgain, wup, wp)
    words, scales = planes(R_out)
    return R_out, words, scales

import math
from contextlib import ExitStack

import concourse.mybir as mybir
from concourse.masks import make_identity

T, D, E, R, F = 1024, 512, 4, 512, 512
FLOPS = 2 * T * E * (D * R + R * F + D * F)

F32 = mybir.dt.float32
BF16 = mybir.dt.bfloat16
U32 = mybir.dt.uint32
I32 = mybir.dt.int32
U8 = mybir.dt.uint8
FP8X4 = mybir.dt.float8_e4m3fn_x4
ALU = mybir.AluOpType
ACT = mybir.ActivationFunctionType
AX = mybir.AxisListType

P = 128
PACK = 4
GROUP = 512
LOG2E = math.log2(math.e)


def tile_autonomyofexpertsnormgate_x1_kernel(tc, x, wdown, rgain, wup, wp, out_0, out_1, out_2):
    nc = tc.nc
    G = T // GROUP
    PAIRS = G * E * 2
    LEAD = 18
    VADDS = (2, 5, 10, 12, 14, 15, )
    SB = ()
    CLUSTERS = (5, 7, 9, 11, 13, 99, )

    with ExitStack() as ctx:
        keep = ctx.enter_context(tc.tile_pool(name="keep", bufs=1))
        work = ctx.enter_context(tc.tile_pool(name="work", bufs=3))
        psum = ctx.enter_context(tc.psum_pool(name="psum", bufs=4))
        ctx.enter_context(tc.manual_schedule())
        gain = keep.tile([P, E, 16], BF16, name="gain")
        ident = keep.tile([P, P], F32, name="ident")
        ident_b = keep.tile([P, P], BF16, name="ident_b")
        gain32 = keep.tile([P, E, PACK], F32, name="gain32")
        half = keep.tile([P, 16], F32, name="half")
        two = keep.tile([P, 16], F32, name="two")
        minus = keep.tile([P, 4], F32, name="minus")
        warm = keep.tile([P, 1], F32, name="warm")
        x_raw = [keep.tile([P, PACK, D], BF16, name="x_raw%d" % g, align_bytes=64) for g in range(G)]
        names = ["wd%d" % e for e in range(E)] + ["wp%d" % e for e in range(E)] + ["wu%d" % e for e in range(E)]
        raw = {n: keep.tile([P, PACK, 512], BF16, name="raw_" + n, align_bytes=64) for n in names}
        xc = [keep.tile([P, GROUP], U32, name="xc%d" % g, align_bytes=64) for g in range(G)]
        xs = [keep.tile([P, GROUP], U8, name="xs%d" % g, align_bytes=64) for g in range(G)]
        dcodes = [keep.tile([P, 512], U32, name="dcodes%d" % e, align_bytes=64) for e in range(E)]
        dscales = [keep.tile([P, 512], U8, name="dscales%d" % e, align_bytes=64) for e in range(E)]
        dgrp = [keep.tile([P, 512, PACK], BF16, name="dgrp%d" % e, align_bytes=64) for e in range(E)]
        pcodes = [keep.tile([P, 2, 512], U32, name="pcodes%d" % e, align_bytes=64) for e in range(E)]
        pscales = [keep.tile([P, 2, 512], U8, name="pscales%d" % e, align_bytes=64) for e in range(E)]
        pgrp = [keep.tile([P, 2, 512, PACK], BF16, name="pgrp%d" % e, align_bytes=64) for e in range(E)]
        sumsq = [keep.tile([P, PACK, E], F32, name="sumsq%d" % g) for g in range(G)]
        gate = [keep.tile([P, PACK, E], F32, name="gate%d" % g) for g in range(G)]
        acc = [keep.tile([P, PACK, F], F32, name="acc%d" % g) for g in range(G)]

        src = {}
        for e in range(E):
            src["wd%d" % e] = wdown[e]
            src["wp%d" % e] = wp[e]
            src["wu%d" % e] = wup[e]

        nc.scalar.dma_start(out=gain[:, :, 0:PACK], in_=rgain.rearrange("e (p t) -> p e t", t=PACK))

        def load_x(g):
            nc.sync.dma_start(out=x_raw[g][:], in_=x[g * GROUP:(g + 1) * GROUP, :].rearrange("(p t) d -> p t d", t=PACK))

        def load_w(n):
            nc.sync.dma_start(out=raw[n][:], in_=src[n].rearrange("(p j) c -> p j c", j=PACK))

        load_w("wd0")
        load_x(0)
        for n in ("wd1", "wd2", "wd3", "wp0", "wu0"):
            load_w(n)
        load_x(1)
        for n in ("wp1", "wu1", "wp2", "wu2", "wp3", "wu3"):
            load_w(n)

        nc.vector.memset(warm[:], 0.0)
        nc.scalar.activation(out=warm[:], in_=warm[:], func=ACT.Silu)
        nc.vector.tensor_copy(out=gain32[:], in_=gain[:, :, 0:PACK])
        make_identity(nc, ident[:])
        nc.gpsimd.tensor_copy(out=ident_b[:], in_=ident[:])
        nc.gpsimd.memset(half[:], 0.5)
        nc.gpsimd.memset(two[:], 2.0)
        nc.gpsimd.memset(minus[:], -1.0)

        def copy_on(eng, out, in_):
            if eng == "V":
                nc.vector.tensor_copy(out=out, in_=in_)
            elif eng == "S":
                nc.scalar.copy(out=out, in_=in_)
            else:
                nc.gpsimd.tensor_scalar(out=out, in0=in_, scalar1=1.0, scalar2=0.0, op0=ALU.mult, op1=ALU.add)

        def ilv(n, eng, lo=0, hi=4):
            e = int(n[2:])
            if n.startswith("wd"):
                copy_on(eng, dgrp[e][:].rearrange("p (t m) j -> p t m j", t=4)[:, lo:hi],
                        raw[n][:].rearrange("p j (m t) -> p t m j", t=4)[:, lo:hi])
            else:
                w = 0 if n.startswith("wp") else 1
                copy_on(eng, pgrp[e][:, w, 128 * lo:128 * hi, :], raw[n][:, :, 128 * lo:128 * hi].rearrange("p j c -> p c j"))

        banks = {}

        def pe_turn(n, h):
            bank = psum.tile([P, 1024], BF16, name="pw", tag="ps", bufs=4)
            banks[n, h] = bank
            for q in range(2):
                c0 = 256 * h + 128 * q
                nc.tensor.matmul(out=bank[:, 512 * q:512 * (q + 1)].rearrange("p (m j) -> p m j", j=PACK), lhsT=ident_b[:],
                                 rhs=raw[n][:, :, c0:c0 + 128].rearrange("p j m -> p m j"), start=True, stop=True)

        def pe_out(n, h):
            w = 0 if n.startswith("wp") else 1
            nc.scalar.copy(out=pgrp[int(n[2:])][:, w, 256 * h:256 * (h + 1), :].rearrange("p m j -> p (m j)"), in_=banks[n, h][:])

        def quant_d(e):
            nc.vector.quantize_mx(out=dcodes[e][:].bitcast(FP8X4), scales=dscales[e][:],
                                  in_=dgrp[e][:].rearrange("p c j -> p (c j)"))

        def quant_p(e):
            nc.vector.quantize_mx(out=pcodes[e][:].rearrange("p w c -> p (w c)").bitcast(FP8X4),
                                  scales=pscales[e][:].rearrange("p w c -> p (w c)"),
                                  in_=pgrp[e][:].rearrange("p w c j -> p (w c j)"))

        xg = {}

        def x_turn(g, engs):
            xg[g] = work.tile([P, GROUP, PACK], BF16, name="xgrp", align_bytes=64, bufs=1)
            words = x_raw[g][:].rearrange("p t d -> p (t d)").bitcast(F32)
            dstw = xg[g][:].rearrange("p c j -> p (c j)").bitcast(F32).rearrange("p (s r u) -> p s r u", r=P, u=2)
            for h in range(2):
                bank = psum.tile([P, 512], F32, name="pt", tag="ps", bufs=4)
                view = bank[:].rearrange("p (s u r) -> p s u r", s=2, u=2)
                for s in range(2):
                    t = 2 * h + s
                    for u in range(2):
                        nc.tensor.transpose(view[:, s, u, :], words[:, 256 * t + u:256 * (t + 1):2], ident[:])
                copy_on(engs[h], dstw[:, 2 * h:2 * h + 2], view.rearrange("p s u r -> p s r u"))

        def x_quant(g):
            nc.vector.quantize_mx(out=xc[g][:].bitcast(FP8X4), scales=xs[g][:],
                                  in_=xg[g][:].rearrange("p c j -> p (c j)"))

        bgrp = {}
        bcodes = {}
        bscales = {}

        def cols(t):
            return slice(P * t, P * (t + 1))

        def a_pair(i):
            g, e, h = i // 8, (i // 2) % 4, i % 2
            ts = (2 * h, 2 * h + 1)
            wc, ws = dcodes[e], dscales[e]
            ar = {}
            at = {}
            for t in ts:
                arb = psum.tile([P, 512], F32, name="pa", tag="pv", bufs=4)
                ar[t] = arb[:].rearrange("p (k n) -> p k n", k=4)
                for k in range(4):
                    nc.tensor.matmul_mx(out=ar[t][:, k, :], lhsT=wc[:, cols(k)].bitcast(FP8X4), lhsT_scale=ws[:, cols(k)],
                                        rhs=xc[g][:, cols(t)].bitcast(FP8X4), rhs_scale=xs[g][:, cols(t)],
                                        start=True, stop=True)
            for t in ts:
                atb = psum.tile([P, 512], F32, name="pb", tag="ps", bufs=4)
                at[t] = atb
                nc.tensor.matmul_mx(out=atb[:], lhsT=xc[g][:, cols(t)].bitcast(FP8X4), lhsT_scale=xs[g][:, cols(t)],
                                    rhs=wc[:].bitcast(FP8X4), rhs_scale=ws[:], start=True, stop=True)
            if h == 0:
                bgrp[g, e] = work.tile([P, GROUP, PACK], BF16, name="bgrp", align_bytes=64, bufs=3)
            for t in reversed(ts):
                sq = work.tile([P, 512], F32, name="sq", bufs=2)
                nc.scalar.activation(out=sq[:], in_=at[t][:], func=ACT.Square, accum_out=sumsq[g][:, t, e:e + 1])
            for t in reversed(ts):
                if 2 * i + t % 2 in SB:
                    for k in range(4):
                        nc.scalar.activation(out=bgrp[g, e][:, cols(t), k], in_=ar[t][:, k, :], func=ACT.Copy,
                                             scale=gain32[:, e, k:k + 1])
                    continue
                nc.vector.tensor_tensor(out=bgrp[g, e][:, cols(t), :], in0=ar[t].rearrange("p k n -> p n k"),
                                        in1=gain[:, e, 0:PACK].unsqueeze(1).to_broadcast([P, P, PACK]), op=ALU.mult)

        def b_quant(g, e):
            bcodes[g, e] = keep.tile([P, GROUP], U32, name="bc%d%d" % (g, e), align_bytes=64)
            bscales[g, e] = keep.tile([P, GROUP], U8, name="bs%d%d" % (g, e), align_bytes=64)
            nc.vector.quantize_mx(out=bcodes[g, e][:].bitcast(FP8X4), scales=bscales[g, e][:],
                                  in_=bgrp[g, e][:].rearrange("p c j -> p (c j)"))

        soft = {}

        def soft_step(g, k):
            if k == 0:
                soft["sc", g] = keep.tile([P, PACK, E], F32, name="sc%d" % g)
                soft["mx", g] = keep.tile([P, PACK], F32, name="mx%d" % g)
                soft["ex", g] = keep.tile([P, PACK, E], F32, name="ex%d" % g)
                soft["s2", g] = keep.tile([P, PACK, 2], F32, name="s2%d" % g)
                soft["sm", g] = keep.tile([P, PACK], F32, name="sm%d" % g)
                nc.gpsimd.tensor_tensor(out=soft["sc", g][:].rearrange("p t e -> p (t e)"),
                                        in0=sumsq[g][:].rearrange("p t e -> p (t e)"), in1=half[:], op=ALU.pow)
                nc.gpsimd.tensor_scalar(out=soft["sc", g][:], in0=soft["sc", g][:], scalar1=LOG2E, scalar2=0.0,
                                        op0=ALU.mult, op1=ALU.add)
            elif k == 1:
                nc.vector.tensor_reduce(out=soft["mx", g][:], in_=soft["sc", g][:], axis=AX.X, op=ALU.max)
            else:
                ex = soft["ex", g]
                nc.gpsimd.tensor_tensor(out=soft["sc", g][:], in0=soft["sc", g][:],
                                        in1=soft["mx", g][:].unsqueeze(2).to_broadcast([P, PACK, E]), op=ALU.subtract)
                nc.gpsimd.tensor_tensor(out=ex[:].rearrange("p t e -> p (t e)"), in0=two[:],
                                        in1=soft["sc", g][:].rearrange("p t e -> p (t e)"), op=ALU.pow)
                nc.gpsimd.tensor_tensor(out=soft["s2", g][:], in0=ex[:, :, 0:2], in1=ex[:, :, 2:4], op=ALU.add)
                nc.gpsimd.tensor_tensor(out=soft["sm", g][:], in0=soft["s2", g][:, :, 0], in1=soft["s2", g][:, :, 1], op=ALU.add)
                nc.gpsimd.tensor_tensor(out=soft["mx", g][:], in0=soft["sm", g][:], in1=minus[:], op=ALU.pow)
                nc.gpsimd.tensor_tensor(out=gate[g][:], in0=ex[:], in1=soft["mx", g][:].unsqueeze(2).to_broadcast([P, PACK, E]),
                                        op=ALU.mult)

        ypair = {}

        def b_pair(i):
            g, e, h = i // 8, (i // 2) % 4, i % 2
            ts = (2 * h, 2 * h + 1)
            pps = {}
            ups = {}
            for t in ts:
                pb_ = psum.tile([P, 512], F32, name="pp", tag="pv", bufs=4)
                pps[t] = pb_
                nc.tensor.matmul_mx(out=pb_[:], lhsT=xc[g][:, cols(t)].bitcast(FP8X4), lhsT_scale=xs[g][:, cols(t)],
                                    rhs=pcodes[e][:, 0, :].bitcast(FP8X4), rhs_scale=pscales[e][:, 0, :], start=True, stop=True)
            for t in ts:
                ub_ = psum.tile([P, 512], F32, name="pu", tag="ps", bufs=4)
                ups[t] = ub_
                nc.tensor.matmul_mx(out=ub_[:], lhsT=bcodes[g, e][:, cols(t)].bitcast(FP8X4), lhsT_scale=bscales[g, e][:, cols(t)],
                                    rhs=pcodes[e][:, 1, :].bitcast(FP8X4), rhs_scale=pscales[e][:, 1, :], start=True, stop=True)
            sl = work.tile([P, 2, F], F32, name="sl", bufs=3)
            if e > 0:
                ypair[i] = work.tile([P, 2, F], F32, name="y", bufs=4)
            for t in reversed(ts):
                nc.scalar.activation(out=sl[:, t - 2 * h, :], in_=ups[t][:], func=ACT.Silu)
            for t in ts:
                dst = acc[g][:, t, :] if e == 0 else ypair[i][:, t - 2 * h, :]
                nc.vector.scalar_tensor_tensor(out=dst, in0=pps[t][:], scalar=gate[g][:, t, e:e + 1], in1=sl[:, t - 2 * h, :],
                                               op0=ALU.mult, op1=ALU.mult)

        summed = {}

        def b_add(i):
            g, e, h = i // 8, (i // 2) % 4, i % 2
            if e == 0:
                return
            half_ = acc[g][:, 2 * h:2 * h + 2, :]
            eng = nc.vector if i in VADDS else nc.gpsimd
            eng.tensor_tensor(out=half_, in0=half_, in1=ypair[i][:], op=ALU.add)
            summed[g, h] = summed.get((g, h), 0) + 1
            if summed[g, h] == E - 1:
                nc.sync.dma_start(out=out_0[g * GROUP:(g + 1) * GROUP, :].rearrange("(p t) f -> p t f", t=PACK)[:, 2 * h:2 * h + 2, :],
                                  in_=half_)

        og = {}
        oc = {}
        osc = {}

        def o_ilv(g, eng, lo, hi):
            assert all(summed[g, h] == E - 1 for h in range(2))
            if g not in og:
                og[g] = work.tile([P, F, PACK], BF16, name="og", align_bytes=64, bufs=1)
            copy_on(eng, og[g][:, lo:hi, :], acc[g][:].rearrange("p t f -> p f t")[:, lo:hi, :])

        def o_quant(g):
            oc[g] = keep.tile([P, F], U32, name="oc%d" % g, align_bytes=64)
            osc[g] = keep.tile([P, F], U8, name="osc%d" % g, align_bytes=64)
            nc.vector.quantize_mx(out=oc[g][:].bitcast(FP8X4), scales=osc[g][:],
                                  in_=og[g][:].rearrange("p c j -> p (c j)"))
            nc.sync.dma_start(out=out_1[g].rearrange("p m b -> p (m b)").bitcast(I32), in_=oc[g][:].bitcast(I32))
            for q in range(4):
                nc.sync.dma_start(out=out_2[g, 4 * q:4 * q + 4, :].bitcast(I32),
                                  in_=osc[g][32 * q:32 * q + 4, :].bitcast(I32))

        ilv("wd0", "S", 3, 4)
        ilv("wd0", "V", 0, 3)
        x_turn(0, ("S", "S"))
        quant_d(0)
        ilv("wd1", "V", 0, 2)
        x_quant(0)
        ilv("wd1", "V", 2, 4)

        jobs = {}
        for s, kind, n, h in (
            (-1, 'G', 'wd3', 1),
            (-1, 'G', 'wd3', 0),
            (-1, 'S', 'wd2', 0),
            (-1, 'G', 'wp1', 1),
            (-1, 'S', 'wd2', 1),
            (0, 'G', 'wp1', 0),
            (0, 'S', 'wp0', 0),
            (1, 'QD', 1, 0),
            (1, 'QD', 3, 0),
            (1, 'XT', 1, 0),
            (1, 'QD', 2, 0),
            (2, 'G', 'wp2', 0),
            (3, 'G', 'wu2', 1),
            (3, 'G', 'wp2', 1),
            (4, 'XQ', 1, 0),
            (4, 'G', 'wu0', 1),
            (5, 'G', 'wu2', 0),
            (6, 'S', 'wu1', 1),
            (6, 'S', 'wp0', 1),
            (7, 'S', 'wu1', 0),
            (9, 'SM', 0, 0),
            (9, 'S', 'wu0', 0),
            (10, 'SM', 0, 1),
            (10, 'G', 'wu3', 1),
            (14, 'QP', 0, 0),
            (15, 'SM', 0, 2),
            (15, 'SM', 1, 0),
            (15, 'QP', 1, 0),
            (16, 'S', 'wp3', 0),
            (17, 'SM', 1, 1),
            (19, 'SM', 1, 2),
            (19, 'S', 'wp3', 1),
            (19, 'QP', 2, 0),
            (21, 'G', 'wu3', 0),
            (21, 'QP', 3, 0),
            (27, 'OI', 'G', 2),
            (29, 'OI', 'S', 0),
            (31, 'OI', 'S', 3),
            (31, 'OI', 'S', 1),
            (31, 'OQ', 0, 0),
        ):
            jobs.setdefault(s, []).append((kind, n, h))

        def do_job(kind, n, h):
            if kind == "QD":
                quant_d(n)
            elif kind == "QP":
                quant_p(n)
            elif kind == "XT":
                x_turn(1, ("S", "S"))
            elif kind == "XQ":
                x_quant(1)
            elif kind == "SM":
                soft_step(n, h)
            elif kind == "OI":
                o_ilv(0, n, 128 * h, 128 * (h + 1))
            elif kind == "OQ":
                o_quant(0)
            elif kind == "PE":
                pe_turn(n, h)
            elif kind == "ES":
                pe_out(n, h)
            else:
                ilv(n, kind, 2 * h, 2 * h + 2)

        added = set()

        def flush(k):
            for i in range(PAIRS):
                if i not in added and (i <= k - 1 and k in CLUSTERS if i in VADDS else i <= k - 1):
                    added.add(i)
                    b_add(i)

        for s in range(-1, PAIRS + LEAD):
            if 0 <= s < PAIRS:
                a_pair(s)
            if s > 0 and s % 2 == 0 and s <= PAIRS:
                b_quant((s // 2 - 1) // E, (s // 2 - 1) % E)
            k = s - LEAD
            for job in jobs.get(s, []):
                if job[0] == "SM":
                    do_job(*job)
            if k >= 0:
                b_pair(k)
                flush(k)
            for job in jobs.get(s, []):
                if job[0] != "SM":
                    do_job(*job)
        flush(99)
        o_ilv(1, "S", 352, 512)
        o_ilv(1, "V", 0, 352)
        o_quant(1)
